import numpy as np, ml_dtypes
CORES = [2,42,66,74,82,90,114]
N = 7
import mx_ref
NC, KB = 256, 1
BF = ml_dtypes.bfloat16
def cut(t, i, w=512):
    return t[:, w * i:w * i + w]
def term(a, B):
    return np.stack([mx_ref.matmul(mx_ref.quantize(cut(a, i)), B) for i in range(4)], axis=2).reshape(128, -1)
def setup_inputs(rng):
    def f(*shape):
        return mx_ref.flush((rng.standard_normal(shape, dtype=np.float32) * np.exp2(rng.integers(-2, 3, shape[:-1] + (1,)))).astype(BF))
    return {"a": f(N, 128, 4 * 512), "b": f(N, 128, KB * 4 * NC)}
def setup_inputs_blocks(rng):
    d = setup_inputs(rng)
    for k in ("a", "b"): d[k] = mx_ref.spread(d[k], rng, 2)
    return d
def setup_inputs_wide(rng):
    d = setup_inputs(rng)
    for k in ("a", "b"): d[k] = mx_ref.flush((d[k].astype(np.float32) * np.exp2(rng.integers(-4, 5, (N, 1, 1))).astype(np.float32)).astype(BF))
    return d
def setup_inputs_lossless(rng):
    a = np.zeros((N, 128, 4 * 128, 4), np.float32)
    for r in range(N):
        k = rng.integers(0, 512, size=4 * 128)
        a[r, k // 4, np.arange(4 * 128), k % 4] = 1.0
    size = np.repeat(2.0 ** rng.integers(-4, 5, size=(1, 1, (KB * 4 * NC) // 4)), 4, axis=2)
    b = rng.integers(-1, 2, size=(N, 128, KB * 4 * NC)) * size
    return {"a": a.reshape(N, 128, 4 * 512).astype(BF), "b": b.astype(np.float32).astype(BF)}
def reference(a, b):
    y = np.zeros((N, 128, KB * 4 * NC), np.float32)
    for k in range(KB):
        y[:, :, 4 * NC * k:4 * NC * k + 4 * NC] = mx_ref.total([term(a[r], mx_ref.quantize(cut(b[r], k, 4 * NC))) for r in range(N)])
    return {"y": y}

@@ -1,0 +1,197 @@
+from concourse.bass import DstId, RemoteDMATransfer
+from concourse.mybir import dt, AluOpType, ActivationFunctionType
+
+N = 7
+NW = 256
+HW = 128
+DIRECT = 6
+HELPED = ()
+
+X4 = "float8_e4m3fn_x4"
+SCRATCH = {
+    "a_sb": ("sbuf", [128, 2048], "bfloat16"),
+    "b_sb": ("sbuf", [128, 1024], "bfloat16"),
+    "aq": ("sbuf", [128, 512], X4), "ap": ("sbuf", [128, 512], "uint8"),
+    "bq": ("sbuf", [128, NW], X4), "bp": ("sbuf", [128, NW], "uint8"),
+    "z": ("sbuf", [128, 516], "bfloat16"),
+    "eq": ("sbuf", [128, 512], X4), "ep": ("sbuf", [128, 512], "uint8"),
+    "tt": ("sbuf", [128, 4 * NW], "bfloat16"),
+    "tq": ("sbuf", [128, NW], X4), "tp": ("sbuf", [128, NW], "uint8"),
+    "lq": ("sbuf", [128, N * NW], X4), "lp": ("sbuf", [128, N * NW], "uint8"),
+    "ps": ("psum", [128, 8 * 512], "float32"),
+    "yy": ("sbuf", [128, 4 * NW], "float32"),
+}
+SEMAPHORES = (["ldb", "lda0", "lda1", "ones", "diag", "qb", "qe", "cp0", "cp1", "tqs", "sent", "hp", "hq",
+               "y0", "y1", "st"]
+              + ["qa%d" % i for i in range(4)] + ["p%d" % k for k in range(8)] + ["d%d" % k for k in range(8)]
+              + ["arr%d" % r for r in range(N)])
+
+
+def _count(m):
+    return bin(m).count("1")
+
+
+def _common(topo, src, dsts):
+    m = topo.mask(src, dsts[0])
+    for d in dsts[1:]:
+        m &= topo.mask(src, d)
+    return m
+
+
+def _roads(T, topo, r):
+    me = T.cores[r]
+    order = [(r + k) % N for k in range(1, N)]
+    roads = [(me, order[:DIRECT])]
+    rest = order[DIRECT:]
+    if rest:
+        near = [c for c in range(topo.CHIPS * topo.CORES_PER_CHIP)
+                if topo.chip(c) == topo.chip(me) and T.rank_of(c) is None
+                and all(topo.may_write(c, T.cores[q]) for q in order)]
+        near.sort(key=lambda c: topo.die(c) == topo.die(me))
+        for k, n in enumerate(HELPED):
+            roads.append((near[k], rest[:n]))
+            rest = rest[n:]
+    return roads
+
+
+def _xfer(topo, dsts, mask, sem, src, dst):
+    ids = [DstId(rid=topo.addr(c)[0], pnc=topo.addr(c)[1]) for c in dsts]
+    return RemoteDMATransfer(dst_ids=ids, dma_engine_mask=mask, remote_sem=sem, srcs=[src], dsts=[dst] * len(ids))
+
+
+def _plane(T, r):
+    return T.lp[:, NW * r:NW * r + NW]
+
+
+def _codes(T, r):
+    return T.lq[:, NW * r:NW * r + NW].bitcast(dt.uint8)
+
+
+def _relay(g, core, T, topo, r, owners, n_in):
+    far = [T.cores[q] for q in owners]
+    fm = _common(topo, core, far)
+    g.wait_ge(T.sem.hp, n_in)
+    g.remote_dma_fused([_xfer(topo, far, fm, T.sem["arr%d" % r], T.tp[:, :], _plane(T, r))], local_sem=T.sem.sent)
+    g.wait_ge(T.sem.hq, n_in)
+    g.remote_dma_fused([_xfer(topo, far, fm, T.sem["arr%d" % r], T.tq[:, :].bitcast(dt.uint8), _codes(T, r))],
+                       local_sem=T.sem.sent)
+    g.wait_ge(T.sem.sent, 2 * _count(fm))
+
+
+def _masks(T, topo, r):
+    roads = _roads(T, topo, r)
+    me = roads[0][0]
+    far = [T.cores[q] for q in roads[0][1]]
+    near = [c for c, o in roads[1:]]
+    fm = _common(topo, me, far) if far else 0
+    nm = (_common(topo, me, near) & ~fm) if near else 0
+    return far, near, fm, nm
+
+
+def rank_program(g, core, T, topo):
+    r = T.rank_of(core)
+    if r is None:
+        for s in range(N):
+            for c, owners in _roads(T, topo, s)[1:]:
+                if c == core:
+                    _relay(g, core, T, topo, s, owners, _count(_masks(T, topo, s)[3]))
+        return
+    S, v, te, sc, sy = T.sem, g.vector, g.tensor, g.scalar, g.sync
+    Copy = ActivationFunctionType.Copy
+
+    def bank(h, i):
+        k = 512 * (4 * h + i)
+        return T.ps[:, k:k + HW]
+
+    def stripe(buf, h, i):
+        return buf[:, 4 * HW * h + i:4 * HW * (h + 1):4]
+
+    sy.dma_start(T.b_sb[:, :], T.b[:, :]).then_inc(S.ldb, 16)
+    sc.dma_start(T.a_sb[:, 0:1024], T.a[:, 0:1024]).then_inc(S.lda0, 16)
+    sy.dma_start(T.a_sb[:, 1024:2048], T.a[:, 1024:2048]).then_inc(S.lda1, 16)
+
+    v.memset(T.z[:, :], 1.0).then_inc(S.ones, 1)
+    g.wait_ge(S.ones, 1)
+    g.affine_select(T.z[:, :], T.z[:, :], [[1, 516]], AluOpType.is_equal, 0.0, -3, -4).then_inc(S.diag, 1)
+
+    v.wait_ge(S.ldb, 16)
+    v.quantize_mx(T.bq[:, :], T.bp[:, :], T.b_sb[:, :]).then_inc(S.qb, 1)
+    for i in range(4):
+        if i % 2 == 0:
+            v.wait_ge(S["lda%d" % (i // 2)], 16)
+        v.quantize_mx(T.aq[:, HW * i:HW * i + HW], T.ap[:, HW * i:HW * i + HW],
+                      T.a_sb[:, 512 * i:512 * i + 512]).then_inc(S["qa%d" % i], 1)
+
+    def product(h, i, stop):
+        return te.matmul_mx(bank(h, i), T.aq[:, HW * i:HW * i + HW], T.ap[:, HW * i:HW * i + HW],
+                            T.bq[:, HW * h:HW * h + HW], T.bp[:, HW * h:HW * h + HW], True, stop)
+
+    te.wait_ge(S.qb, 1)
+    for i in range(4):
+        te.wait_ge(S["qa%d" % i], 1)
+        for h in range(2):
+            product(h, i, True).then_inc(S["p%d" % (4 * h + i)], 1)
+
+    for i in range(4):
+        for h in range(2):
+            if (i, h) == (3, 0):
+                continue
+            sc.wait_ge(S["p%d" % (4 * h + i)], 1)
+            sc.activation(stripe(T.tt, h, i), bank(h, i), Copy).then_inc(S["cp%d" % h], 1)
+    v.wait_ge(S.p3, 1)
+    v.tensor_copy(stripe(T.tt, 0, 3), bank(0, 3)).then_inc(S.cp0, 1)
+    for h in range(2):
+        v.wait_ge(S["cp%d" % h], 4)
+        v.quantize_mx(T.tq[:, HW * h:HW * h + HW], T.tp[:, HW * h:HW * h + HW],
+                      T.tt[:, 4 * HW * h:4 * HW * (h + 1)]).then_inc(S.tqs, 1)
+
+    far, near, fm, nm = _masks(T, topo, r)
+    g.wait_ge(S.tqs, 2)
+    for src, here, there, hs in ((T.tp[:, :], T.tp[:, :], _plane(T, r), S.hp),
+                                 (T.tq[:, :].bitcast(dt.uint8), T.tq[:, :].bitcast(dt.uint8), _codes(T, r), S.hq)):
+        tr = []
+        if near:
+            tr.append(_xfer(topo, near, nm, hs, src, here))
+        if far:
+            tr.append(_xfer(topo, far, fm, S["arr%d" % r], src, there))
+        g.remote_dma_fused(tr, local_sem=S.sent)
+
+    v.wait_ge(S.diag, 1)
+    for t in range(4):
+        v.quantize_mx(T.eq[:, HW * t:HW * t + HW], T.ep[:, HW * t:HW * t + HW],
+                      T.z[:, 3 - t:3 - t + 512]).then_inc(S.qe, 1)
+
+    te.wait_ge(S.cp0, 4)
+    te.wait_ge(S.cp1, 4)
+    for h in range(2):
+        for i in range(4):
+            product(h, i, False)
+
+    te.wait_ge(S.qe, 4)
+    for k in range(1, N):
+        s = (r - k) % N
+        n_in = 0
+        for c, owners in _roads(T, topo, s):
+            if r in owners:
+                n_in = 2 * _count(_common(topo, c, [T.cores[q] for q in owners]))
+        te.wait_ge(S["arr%d" % s], n_in)
+        for h in range(2):
+            lo = NW * s + HW * h
+            for t in range(4):
+                mm = te.matmul_mx(bank(h, t), T.eq[:, HW * t:HW * t + HW], T.ep[:, HW * t:HW * t + HW],
+                                  T.lq[:, lo:lo + HW], T.lp[:, lo:lo + HW], False, k == N - 1)
+                if k == N - 1:
+                    mm.then_inc(S["d%d" % (4 * h + t)], 1)
+
+    for h in range(2):
+        for t in range(4):
+            if t % 2 == 0:
+                v.wait_ge(S["d%d" % (4 * h + t)], 1)
+                v.tensor_copy(stripe(T.yy, h, t), bank(h, t)).then_inc(S["y%d" % h], 1)
+            else:
+                sc.wait_ge(S["d%d" % (4 * h + t)], 1)
+                sc.activation(stripe(T.yy, h, t), bank(h, t), Copy).then_inc(S["y%d" % h], 1)
+        sy.wait_ge(S["y%d" % h], 4)
+        sy.dma_start(T.y[:, 512 * h:512 * h + 512], T.yy[:, 512 * h:512 * h + 512]).then_inc(S.st, 16)
+    sy.wait_ge(S.st, 32)
+    g.wait_ge(S.sent, 2 * (_count(fm) + _count(nm)))

@@ -4,8 +4,8 @@ from concourse.mybir import dt, AluOpType, ActivationFunctionType
 N = 7
 NW = 256
 HW = 128
-DIRECT = 6
-HELPED = ()
+DIRECT = 3
+HELPED = (2, 1)
 
 X4 = "float8_e4m3fn_x4"
 SCRATCH = {

@@ -21,10 +21,10 @@ SCRATCH = {
     "ps": ("psum", [128, 8 * 512], "float32"),
     "yy": ("sbuf", [128, 4 * NW], "float32"),
 }
-SEMAPHORES = (["ldb", "lda0", "lda1", "ones", "diag", "qb", "qe", "cp0", "cp1", "tqs", "sent", "hp", "hq",
-               "y0", "y1", "st"]
+SEMAPHORES = (["ldb0", "ldb1", "lda0", "lda2", "lda3", "ones", "diag", "qb0", "qb1", "qe", "cp0", "cp1", "tq0", "tq1",
+               "sent", "hp", "hq0", "hq1", "y0", "y1", "st"]
               + ["qa%d" % i for i in range(4)] + ["p%d" % k for k in range(8)] + ["d%d" % k for k in range(8)]
-              + ["arr%d" % r for r in range(N)])
+              + ["arr%d" % r for r in range(N)] + ["brr%d" % r for r in range(N)])
 
 
 def _count(m):
@@ -59,23 +59,23 @@ def _xfer(topo, dsts, mask, sem, src, dst):
     return RemoteDMATransfer(dst_ids=ids, dma_engine_mask=mask, remote_sem=sem, srcs=[src], dsts=[dst] * len(ids))
 
 
-def _plane(T, r):
-    return T.lp[:, NW * r:NW * r + NW]
-
-
-def _codes(T, r):
-    return T.lq[:, NW * r:NW * r + NW].bitcast(dt.uint8)
+def _pieces(T, r):
+    def codes(h):
+        return (T.tq[:, HW * h:HW * h + HW].bitcast(dt.uint8),
+                T.lq[:, NW * r + HW * h:NW * r + HW * h + HW].bitcast(dt.uint8))
+    first, second = T.sem["arr%d" % r], T.sem["brr%d" % r]
+    return [codes(0) + (T.sem.hq0, first),
+            (T.tp[:, :], T.lp[:, NW * r:NW * r + NW], T.sem.hp, first),
+            codes(1) + (T.sem.hq1, second)]
 
 
 def _relay(g, core, T, topo, r, owners, n_in):
     far = [T.cores[q] for q in owners]
     fm = _common(topo, core, far)
-    g.wait_ge(T.sem.hp, n_in)
-    g.remote_dma_fused([_xfer(topo, far, fm, T.sem["arr%d" % r], T.tp[:, :], _plane(T, r))], local_sem=T.sem.sent)
-    g.wait_ge(T.sem.hq, n_in)
-    g.remote_dma_fused([_xfer(topo, far, fm, T.sem["arr%d" % r], T.tq[:, :].bitcast(dt.uint8), _codes(T, r))],
-                       local_sem=T.sem.sent)
-    g.wait_ge(T.sem.sent, 2 * _count(fm))
+    for here, there, hs, os in _pieces(T, r):
+        g.wait_ge(hs, n_in)
+        g.remote_dma_fused([_xfer(topo, far, fm, os, here, there)], local_sem=T.sem.sent)
+    g.wait_ge(T.sem.sent, 3 * _count(fm))
 
 
 def _masks(T, topo, r):
@@ -86,6 +86,14 @@ def _masks(T, topo, r):
     fm = _common(topo, me, far) if far else 0
     nm = (_common(topo, me, near) & ~fm) if near else 0
     return far, near, fm, nm
+
+
+def _landing(T, topo, s, r):
+    for k, (c, owners) in enumerate(_roads(T, topo, s)):
+        if r in owners:
+            late = 0 if k == 0 else len(HELPED)
+            return owners.index(r) + late, _count(_common(topo, c, [T.cores[q] for q in owners]))
+    return None
 
 
 def rank_program(g, core, T, topo):
@@ -106,54 +114,69 @@ def rank_program(g, core, T, topo):
     def stripe(buf, h, i):
         return buf[:, 4 * HW * h + i:4 * HW * (h + 1):4]
 
-    sy.dma_start(T.b_sb[:, :], T.b[:, :]).then_inc(S.ldb, 16)
+    sy.dma_start(T.b_sb[:, 0:512], T.b[:, 0:512]).then_inc(S.ldb0, 16)
     sc.dma_start(T.a_sb[:, 0:1024], T.a[:, 0:1024]).then_inc(S.lda0, 16)
-    sy.dma_start(T.a_sb[:, 1024:2048], T.a[:, 1024:2048]).then_inc(S.lda1, 16)
+    sy.dma_start(T.a_sb[:, 1024:1536], T.a[:, 1024:1536]).then_inc(S.lda2, 16)
+    sc.dma_start(T.a_sb[:, 1536:2048], T.a[:, 1536:2048]).then_inc(S.lda3, 16)
+    sy.dma_start(T.b_sb[:, 512:1024], T.b[:, 512:1024]).then_inc(S.ldb1, 16)
 
     v.memset(T.z[:, :], 1.0).then_inc(S.ones, 1)
     g.wait_ge(S.ones, 1)
     g.affine_select(T.z[:, :], T.z[:, :], [[1, 516]], AluOpType.is_equal, 0.0, -3, -4).then_inc(S.diag, 1)
 
-    v.wait_ge(S.ldb, 16)
-    v.quantize_mx(T.bq[:, :], T.bp[:, :], T.b_sb[:, :]).then_inc(S.qb, 1)
-    for i in range(4):
-        if i % 2 == 0:
-            v.wait_ge(S["lda%d" % (i // 2)], 16)
-        v.quantize_mx(T.aq[:, HW * i:HW * i + HW], T.ap[:, HW * i:HW * i + HW],
-                      T.a_sb[:, 512 * i:512 * i + 512]).then_inc(S["qa%d" % i], 1)
+    def pack_b(h):
+        v.wait_ge(S["ldb%d" % h], 16)
+        v.quantize_mx(T.bq[:, HW * h:HW * h + HW], T.bp[:, HW * h:HW * h + HW],
+                      T.b_sb[:, 512 * h:512 * h + 512]).then_inc(S["qb%d" % h], 1)
+
+    def pack_term(h):
+        v.wait_ge(S["cp%d" % h], 4)
+        v.quantize_mx(T.tq[:, HW * h:HW * h + HW], T.tp[:, HW * h:HW * h + HW],
+                      T.tt[:, 4 * HW * h:4 * HW * (h + 1)]).then_inc(S["tq%d" % h], 1)
 
     def product(h, i, stop):
         return te.matmul_mx(bank(h, i), T.aq[:, HW * i:HW * i + HW], T.ap[:, HW * i:HW * i + HW],
                             T.bq[:, HW * h:HW * h + HW], T.bp[:, HW * h:HW * h + HW], True, stop)
 
-    te.wait_ge(S.qb, 1)
+    pack_b(0)
     for i in range(4):
-        te.wait_ge(S["qa%d" % i], 1)
-        for h in range(2):
+        if i != 1:
+            v.wait_ge(S["lda%d" % i], 16)
+        v.quantize_mx(T.aq[:, HW * i:HW * i + HW], T.ap[:, HW * i:HW * i + HW],
+                      T.a_sb[:, 512 * i:512 * i + 512]).then_inc(S["qa%d" % i], 1)
+
+    for h in range(2):
+        te.wait_ge(S["qb%d" % h], 1)
+        for i in range(4):
+            if h == 0:
+                te.wait_ge(S["qa%d" % i], 1)
             product(h, i, True).then_inc(S["p%d" % (4 * h + i)], 1)
 
-    for i in range(4):
-        for h in range(2):
-            if (i, h) == (3, 0):
-                continue
-            sc.wait_ge(S["p%d" % (4 * h + i)], 1)
-            sc.activation(stripe(T.tt, h, i), bank(h, i), Copy).then_inc(S["cp%d" % h], 1)
+    for i in range(3):
+        sc.wait_ge(S["p%d" % i], 1)
+        sc.activation(stripe(T.tt, 0, i), bank(0, i), Copy).then_inc(S.cp0, 1)
     v.wait_ge(S.p3, 1)
     v.tensor_copy(stripe(T.tt, 0, 3), bank(0, 3)).then_inc(S.cp0, 1)
-    for h in range(2):
-        v.wait_ge(S["cp%d" % h], 4)
-        v.quantize_mx(T.tq[:, HW * h:HW * h + HW], T.tp[:, HW * h:HW * h + HW],
-                      T.tt[:, 4 * HW * h:4 * HW * (h + 1)]).then_inc(S.tqs, 1)
+    pack_term(0)
+    pack_b(1)
+    for i in range(4):
+        if i % 2 == 0:
+            sc.wait_ge(S["p%d" % (4 + i)], 1)
+            sc.activation(stripe(T.tt, 1, i), bank(1, i), Copy).then_inc(S.cp1, 1)
+        else:
+            v.wait_ge(S["p%d" % (4 + i)], 1)
+            v.tensor_copy(stripe(T.tt, 1, i), bank(1, i)).then_inc(S.cp1, 1)
+    pack_term(1)
 
     far, near, fm, nm = _masks(T, topo, r)
-    g.wait_ge(S.tqs, 2)
-    for src, here, there, hs in ((T.tp[:, :], T.tp[:, :], _plane(T, r), S.hp),
-                                 (T.tq[:, :].bitcast(dt.uint8), T.tq[:, :].bitcast(dt.uint8), _codes(T, r), S.hq)):
+    for k, (here, there, hs, os) in enumerate(_pieces(T, r)):
+        if k < 2:
+            g.wait_ge(S["tq%d" % k], 1)
         tr = []
         if near:
-            tr.append(_xfer(topo, near, nm, hs, src, here))
+            tr.append(_xfer(topo, near, nm, hs, here, here))
         if far:
-            tr.append(_xfer(topo, far, fm, S["arr%d" % r], src, there))
+            tr.append(_xfer(topo, far, fm, os, here, there))
         g.remote_dma_fused(tr, local_sem=S.sent)
 
     v.wait_ge(S.diag, 1)
@@ -168,19 +191,16 @@ def rank_program(g, core, T, topo):
             product(h, i, False)
 
     te.wait_ge(S.qe, 4)
-    for k in range(1, N):
-        s = (r - k) % N
-        n_in = 0
-        for c, owners in _roads(T, topo, s):
-            if r in owners:
-                n_in = 2 * _count(_common(topo, c, [T.cores[q] for q in owners]))
-        te.wait_ge(S["arr%d" % s], n_in)
-        for h in range(2):
+    senders = sorted([(r - k) % N for k in range(1, N)], key=lambda s: _landing(T, topo, s, r)[0])
+    for h in range(2):
+        for k, s in enumerate(senders):
+            te.wait_ge(S[("arr%d" if h == 0 else "brr%d") % s], (2 - h) * _landing(T, topo, s, r)[1])
+            last = k == len(senders) - 1
             lo = NW * s + HW * h
             for t in range(4):
                 mm = te.matmul_mx(bank(h, t), T.eq[:, HW * t:HW * t + HW], T.ep[:, HW * t:HW * t + HW],
-                                  T.lq[:, lo:lo + HW], T.lp[:, lo:lo + HW], False, k == N - 1)
-                if k == N - 1:
+                                  T.lq[:, lo:lo + HW], T.lp[:, lo:lo + HW], False, last)
+                if last:
                     mm.then_inc(S["d%d" % (4 * h + t)], 1)
 
     for h in range(2):
@@ -194,4 +214,4 @@ def rank_program(g, core, T, topo):
         sy.wait_ge(S["y%d" % h], 4)
         sy.dma_start(T.y[:, 512 * h:512 * h + 512], T.yy[:, 512 * h:512 * h + 512]).then_inc(S.st, 16)
     sy.wait_ge(S.st, 32)
-    g.wait_ge(S.sent, 2 * (_count(fm) + _count(nm)))
+    g.wait_ge(S.sent, 3 * (_count(fm) + _count(nm)))

from concourse.bass import DstId, RemoteDMATransfer
from concourse.mybir import dt, AluOpType, ActivationFunctionType

N = 7
NW = 256
HW = 128
DIRECT = 3
HELPED = (2, 1)

X4 = "float8_e4m3fn_x4"
SCRATCH = {
    "a_sb": ("sbuf", [128, 2048], "bfloat16"),
    "b_sb": ("sbuf", [128, 1024], "bfloat16"),
    "aq": ("sbuf", [128, 512], X4), "ap": ("sbuf", [128, 512], "uint8"),
    "bq": ("sbuf", [128, NW], X4), "bp": ("sbuf", [128, NW], "uint8"),
    "z": ("sbuf", [128, 516], "bfloat16"),
    "eq": ("sbuf", [128, 512], X4), "ep": ("sbuf", [128, 512], "uint8"),
    "tt": ("sbuf", [128, 4 * NW], "bfloat16"),
    "tq": ("sbuf", [128, NW], X4), "tp": ("sbuf", [128, NW], "uint8"),
    "lq": ("sbuf", [128, N * NW], X4), "lp": ("sbuf", [128, N * NW], "uint8"),
    "ps": ("psum", [128, 8 * 512], "float32"),
    "yy": ("sbuf", [128, 4 * NW], "float32"),
}
SEMAPHORES = (["ldb0", "ldb1", "lda0", "lda2", "lda3", "ones", "diag", "qb0", "qb1", "qe", "cp0", "cp1", "tq0", "tq1",
               "sent", "hp", "hq0", "hq1", "y0", "y1", "st"]
              + ["qa%d" % i for i in range(4)] + ["p%d" % k for k in range(8)] + ["d%d" % k for k in range(8)]
              + ["arr%d" % r for r in range(N)] + ["brr%d" % r for r in range(N)])


def _count(m):
    return bin(m).count("1")


def _common(topo, src, dsts):
    m = topo.mask(src, dsts[0])
    for d in dsts[1:]:
        m &= topo.mask(src, d)
    return m


def _roads(T, topo, r):
    me = T.cores[r]
    order = [(r + k) % N for k in range(1, N)]
    roads = [(me, order[:DIRECT])]
    rest = order[DIRECT:]
    if rest:
        near = [c for c in range(topo.CHIPS * topo.CORES_PER_CHIP)
                if topo.chip(c) == topo.chip(me) and T.rank_of(c) is None
                and all(topo.may_write(c, T.cores[q]) for q in order)]
        near.sort(key=lambda c: topo.die(c) == topo.die(me))
        for k, n in enumerate(HELPED):
            roads.append((near[k], rest[:n]))
            rest = rest[n:]
    return roads


def _xfer(topo, dsts, mask, sem, src, dst):
    ids = [DstId(rid=topo.addr(c)[0], pnc=topo.addr(c)[1]) for c in dsts]
    return RemoteDMATransfer(dst_ids=ids, dma_engine_mask=mask, remote_sem=sem, srcs=[src], dsts=[dst] * len(ids))


def _pieces(T, r):
    def codes(h):
        return (T.tq[:, HW * h:HW * h + HW].bitcast(dt.uint8),
                T.lq[:, NW * r + HW * h:NW * r + HW * h + HW].bitcast(dt.uint8))
    first, second = T.sem["arr%d" % r], T.sem["brr%d" % r]
    return [codes(0) + (T.sem.hq0, first),
            (T.tp[:, :], T.lp[:, NW * r:NW * r + NW], T.sem.hp, first),
            codes(1) + (T.sem.hq1, second)]


def _relay(g, core, T, topo, r, owners, n_in):
    far = [T.cores[q] for q in owners]
    fm = _common(topo, core, far)
    for here, there, hs, os in _pieces(T, r):
        g.wait_ge(hs, n_in)
        g.remote_dma_fused([_xfer(topo, far, fm, os, here, there)], local_sem=T.sem.sent)
    g.wait_ge(T.sem.sent, 3 * _count(fm))


def _masks(T, topo, r):
    roads = _roads(T, topo, r)
    me = roads[0][0]
    far = [T.cores[q] for q in roads[0][1]]
    near = [c for c, o in roads[1:]]
    fm = _common(topo, me, far) if far else 0
    nm = (_common(topo, me, near) & ~fm) if near else 0
    return far, near, fm, nm


def _landing(T, topo, s, r):
    for k, (c, owners) in enumerate(_roads(T, topo, s)):
        if r in owners:
            late = 0 if k == 0 else len(HELPED)
            return owners.index(r) + late, _count(_common(topo, c, [T.cores[q] for q in owners]))
    return None


def rank_program(g, core, T, topo):
    r = T.rank_of(core)
    if r is None:
        for s in range(N):
            for c, owners in _roads(T, topo, s)[1:]:
                if c == core:
                    _relay(g, core, T, topo, s, owners, _count(_masks(T, topo, s)[3]))
        return
    S, v, te, sc, sy = T.sem, g.vector, g.tensor, g.scalar, g.sync
    Copy = ActivationFunctionType.Copy

    def bank(h, i):
        k = 512 * (4 * h + i)
        return T.ps[:, k:k + HW]

    def stripe(buf, h, i):
        return buf[:, 4 * HW * h + i:4 * HW * (h + 1):4]

    sy.dma_start(T.b_sb[:, 0:512], T.b[:, 0:512]).then_inc(S.ldb0, 16)
    sc.dma_start(T.a_sb[:, 0:1024], T.a[:, 0:1024]).then_inc(S.lda0, 16)
    sy.dma_start(T.a_sb[:, 1024:1536], T.a[:, 1024:1536]).then_inc(S.lda2, 16)
    sc.dma_start(T.a_sb[:, 1536:2048], T.a[:, 1536:2048]).then_inc(S.lda3, 16)
    sy.dma_start(T.b_sb[:, 512:1024], T.b[:, 512:1024]).then_inc(S.ldb1, 16)

    v.memset(T.z[:, :], 1.0).then_inc(S.ones, 1)
    g.wait_ge(S.ones, 1)
    g.affine_select(T.z[:, :], T.z[:, :], [[1, 516]], AluOpType.is_equal, 0.0, -3, -4).then_inc(S.diag, 1)

    def pack_b(h):
        v.wait_ge(S["ldb%d" % h], 16)
        v.quantize_mx(T.bq[:, HW * h:HW * h + HW], T.bp[:, HW * h:HW * h + HW],
                      T.b_sb[:, 512 * h:512 * h + 512]).then_inc(S["qb%d" % h], 1)

    def pack_term(h):
        v.wait_ge(S["cp%d" % h], 4)
        v.quantize_mx(T.tq[:, HW * h:HW * h + HW], T.tp[:, HW * h:HW * h + HW],
                      T.tt[:, 4 * HW * h:4 * HW * (h + 1)]).then_inc(S["tq%d" % h], 1)

    def product(h, i, stop):
        return te.matmul_mx(bank(h, i), T.aq[:, HW * i:HW * i + HW], T.ap[:, HW * i:HW * i + HW],
                            T.bq[:, HW * h:HW * h + HW], T.bp[:, HW * h:HW * h + HW], True, stop)

    pack_b(0)
    for i in range(4):
        if i != 1:
            v.wait_ge(S["lda%d" % i], 16)
        v.quantize_mx(T.aq[:, HW * i:HW * i + HW], T.ap[:, HW * i:HW * i + HW],
                      T.a_sb[:, 512 * i:512 * i + 512]).then_inc(S["qa%d" % i], 1)

    for h in range(2):
        te.wait_ge(S["qb%d" % h], 1)
        for i in range(4):
            if h == 0:
                te.wait_ge(S["qa%d" % i], 1)
            product(h, i, True).then_inc(S["p%d" % (4 * h + i)], 1)

    for i in range(3):
        sc.wait_ge(S["p%d" % i], 1)
        sc.activation(stripe(T.tt, 0, i), bank(0, i), Copy).then_inc(S.cp0, 1)
    v.wait_ge(S.p3, 1)
    v.tensor_copy(stripe(T.tt, 0, 3), bank(0, 3)).then_inc(S.cp0, 1)
    pack_term(0)
    pack_b(1)
    for i in range(4):
        if i % 2 == 0:
            sc.wait_ge(S["p%d" % (4 + i)], 1)
            sc.activation(stripe(T.tt, 1, i), bank(1, i), Copy).then_inc(S.cp1, 1)
        else:
            v.wait_ge(S["p%d" % (4 + i)], 1)
            v.tensor_copy(stripe(T.tt, 1, i), bank(1, i)).then_inc(S.cp1, 1)
    pack_term(1)

    far, near, fm, nm = _masks(T, topo, r)
    for k, (here, there, hs, os) in enumerate(_pieces(T, r)):
        if k < 2:
            g.wait_ge(S["tq%d" % k], 1)
        tr = []
        if near:
            tr.append(_xfer(topo, near, nm, hs, here, here))
        if far:
            tr.append(_xfer(topo, far, fm, os, here, there))
        g.remote_dma_fused(tr, local_sem=S.sent)

    v.wait_ge(S.diag, 1)
    for t in range(4):
        v.quantize_mx(T.eq[:, HW * t:HW * t + HW], T.ep[:, HW * t:HW * t + HW],
                      T.z[:, 3 - t:3 - t + 512]).then_inc(S.qe, 1)

    te.wait_ge(S.cp0, 4)
    te.wait_ge(S.cp1, 4)
    for h in range(2):
        for i in range(4):
            product(h, i, False)

    te.wait_ge(S.qe, 4)
    senders = sorted([(r - k) % N for k in range(1, N)], key=lambda s: _landing(T, topo, s, r)[0])
    for h in range(2):
        for k, s in enumerate(senders):
            te.wait_ge(S[("arr%d" if h == 0 else "brr%d") % s], (2 - h) * _landing(T, topo, s, r)[1])
            last = k == len(senders) - 1
            lo = NW * s + HW * h
            for t in range(4):
                mm = te.matmul_mx(bank(h, t), T.eq[:, HW * t:HW * t + HW], T.ep[:, HW * t:HW * t + HW],
                                  T.lq[:, lo:lo + HW], T.lp[:, lo:lo + HW], False, last)
                if last:
                    mm.then_inc(S["d%d" % (4 * h + t)], 1)

    for h in range(2):
        for t in range(4):
            if t % 2 == 0:
                v.wait_ge(S["d%d" % (4 * h + t)], 1)
                v.tensor_copy(stripe(T.yy, h, t), bank(h, t)).then_inc(S["y%d" % h], 1)
            else:
                sc.wait_ge(S["d%d" % (4 * h + t)], 1)
                sc.activation(stripe(T.yy, h, t), bank(h, t), Copy).then_inc(S["y%d" % h], 1)
        sy.wait_ge(S["y%d" % h], 4)
        sy.dma_start(T.y[:, 512 * h:512 * h + 512], T.yy[:, 512 * h:512 * h + 512]).then_inc(S.st, 16)
    sy.wait_ge(S.st, 32)
    g.wait_ge(S.sent, 3 * (_count(fm) + _count(nm)))
